import numpy as np
import ml_dtypes


def mxq(x, axis, fmt="e4m3"):
    dtype, down = {"e4m3": (ml_dtypes.float8_e4m3fn, 7), "e5m2": (ml_dtypes.float8_e5m2, 14)}[fmt]
    v = np.moveaxis(np.asarray(x, np.float32).astype(ml_dtypes.bfloat16).astype(np.float64), axis, -1)
    blocks = v.reshape(v.shape[:-1] + (-1, 32))
    amax = np.abs(blocks).max(-1, keepdims=True)
    byte = np.maximum(np.where(amax > 0, np.frexp(amax)[1] - 1 + 127, 0) - down, 1)
    scale = np.exp2(byte - 127.0)
    codes = (blocks / scale).astype(np.float32).astype(dtype).astype(np.float64)
    return np.moveaxis((codes * scale).reshape(v.shape), -1, axis)


WIDE = False


def mx_kscale(k):
    if not WIDE:
        return np.ones(k)
    levels = np.array([10, -10, 5, -5, 0])
    if k % 512:
        return np.exp2(np.random.permutation(np.resize(levels, k // 32))).repeat(32)
    a = np.empty((k // 512, 16))
    for p in range(k // 512):
        a[p, :8] = np.random.permutation(np.resize(levels, 8))
        for g in range(8):
            far = levels[np.abs(levels - a[p, g]) >= 10]
            a[p, g + 8] = far[np.random.randint(len(far))]
    return np.exp2(a.ravel()).repeat(32)


def f64(x):
    return np.asarray(x).astype(np.float64)


def striped(idx):
    return np.tile(idx.reshape(-1, 16).T, (8, 1)).astype(np.uint16)


def unstriped(offs):
    return offs[:16].T.reshape(-1).astype(np.int64)


def striped8(idx):
    return np.concatenate([x.reshape(-1, 16).T for x in idx]).astype(np.uint16)


def runs(offs, k):
    lists = np.stack([offs[16 * r : 16 * r + 16].T.reshape(-1) for r in range(8)]).astype(np.int64)
    return lists[np.arange(k) % 512 // 64]


def pack_weight(w):
    k, n = w.shape
    w = f64(np.asarray(w, np.float32).astype(ml_dtypes.bfloat16)).reshape(k // 32, 32, n)
    amax = np.abs(w).max(1)
    byte = np.clip(np.where(amax > 0, np.frexp(amax)[1] - 1 + 127 - 7, 1), 1, 254)
    scaled = (w * np.exp2(127.0 - byte)[:, None, :]).reshape(k, n).astype(np.float32)
    words = np.ascontiguousarray(scaled.reshape(k // 512, 128, 4, n).transpose(0, 1, 3, 2)).astype(ml_dtypes.float8_e4m3fn).view(np.uint8)
    return words, np.ascontiguousarray(byte.astype(np.uint8).reshape(k // 512, 16, n))


def unpack_weight(words, scales):
    g, p, n, _ = words.shape
    vals = np.ascontiguousarray(words).view(ml_dtypes.float8_e4m3fn).astype(np.float64) * np.repeat(np.exp2(scales.astype(np.float64) - 127.0), 8, axis=1)[..., None]
    return vals.transpose(0, 1, 3, 2).reshape(g * 512, n)


def sigmoid(v):
    return 1.0 / (1.0 + np.exp(-np.maximum(v, -700.0)))


K, T, S, H, J = 512, 2048, 512, 512, 512


def setup_inputs():
    n = np.random.standard_normal
    s = mx_kscale(K)[:, None]
    u = mx_kscale(H)
    packed_xT = pack_weight(n((K, T)) * s)
    return {
        "x_words": packed_xT[0],
        "x_scales": packed_xT[1],
        "w1": (n((K, H)) / np.sqrt(K) / s).astype(np.float32),
        "tab": n((H, J)).astype(np.float32),
        "gn": (np.random.uniform(0.5, 1.5, (H, 1)) * u[:, None]).astype(np.float32),
        "w2": (n((H, H)) / np.sqrt(H) / u[:, None]).astype(np.float32),
        "offs": striped(np.random.permutation(T)[:S]),
        "n1": striped8(np.random.randint(0, J, (8, S))),
        "n2": striped8(np.stack([np.random.permutation(S) for _ in range(8)])),
        "n3": striped8(np.stack([np.random.permutation(S) for _ in range(8)])),
        "n4": striped8(np.stack([np.random.permutation(S) for _ in range(8)])),
        "n5": striped8(np.stack([np.random.permutation(S) for _ in range(8)])),
        "n6": striped8(np.stack([np.random.permutation(S) for _ in range(8)])),
    }


def reference(x_words, x_scales, w1, tab, gn, w2, offs, n1, n2, n3, n4, n5, n6):
    xq = unpack_weight(x_words, x_scales)[:, unstriped(offs)]
    y = mxq(f64(w1), 0, "e4m3").T @ xq
    z = f64(gn) * (np.maximum(y + f64(tab)[np.arange(H)[:, None], runs(n1, H)], y[np.arange(H)[:, None], runs(n2, H)]))
    w2q = mxq(f64(w2), 0, "e4m3")
    a = w2q.T @ mxq(z, 0, "e4m3")
    st = y * (sigmoid(y[np.arange(H)[:, None], runs(n3, H)]))
    z2 = f64(gn) * (st - (st[np.arange(H)[:, None], runs(n4, H)]))
    b = w2q.T @ mxq(z2, 0, "e4m3")
    return (a + a[np.arange(H)[:, None], runs(n5, H)]) * (sigmoid(b + b[np.arange(H)[:, None], runs(n6, H)]))

@@ -1,0 +1,170 @@
+from contextlib import ExitStack
+
+import concourse.mybir as mybir
+
+K, T, S, H = 512, 2048, 512, 512
+FLOPS = 3 * 2 * K * H * S
+
+F32 = mybir.dt.float32
+BF16 = mybir.dt.bfloat16
+I32 = mybir.dt.int32
+U32 = mybir.dt.uint32
+U16 = mybir.dt.uint16
+U8 = mybir.dt.uint8
+FP8X4 = mybir.dt.float8_e4m3fn_x4
+ALU = mybir.AluOpType
+ACT = mybir.ActivationFunctionType
+
+P = 128
+PACK = 4
+WIN = 2 * S
+
+
+def tile_picked_tietriebkindhopg_none_p_kernel(tc, x_words, x_scales, w1, tab, gn, w2, offs, n1, n2, n3, n4, n5, n6, out):
+    nc = tc.nc
+    with ExitStack() as ctx:
+        lists = ctx.enter_context(tc.tile_pool(name="lists", bufs=1))
+        keep = ctx.enter_context(tc.tile_pool(name="keep", bufs=1))
+        psum = ctx.enter_context(tc.psum_pool(name="psum", bufs=1))
+
+        def load_list(name, src):
+            tile = lists.tile([P, S // 16], U16, name=name)
+            nc.sync.dma_start(tile[:], src)
+            return tile
+
+        def tiles(name, width, dtype):
+            return [keep.tile([P, width], dtype, name="%s%d" % (name, t), align_bytes=64) for t in range(PACK)]
+
+        warm = keep.tile([P, 8], F32, name="warm")
+        nc.vector.memset(warm[:, 0:1], 0.0)
+        nc.scalar.activation(warm[:, 1:2], warm[:, 0:1], ACT.Sigmoid)
+
+        x_bytes = keep.tile([P, T], U8, name="x_bytes", align_bytes=64)
+        nc.vector.memset(x_bytes[:].bitcast(I32), 0)
+
+        l1 = load_list("l1", n1)
+        tab_win = tiles("tab_win", WIN, F32)
+        tab_rows = tab.rearrange("(p t) c -> p t c", t=PACK)
+        for t in range(2):
+            nc.sync.dma_start(tab_win[t][:, 0:S], tab_rows[:, t, :])
+        w1_raw = keep.tile([P, PACK, H], F32, name="w1_raw")
+        nc.sync.dma_start(w1_raw[:], w1.rearrange("(p j) c -> p j c", j=PACK))
+        l_offs = load_list("l_offs", offs)
+        for q in range(4):
+            nc.sync.dma_start(x_bytes[32 * q : 32 * q + 4, :].bitcast(I32), x_scales[0, 4 * q : 4 * q + 4, :].bitcast(I32))
+        x_all = keep.tile([P, T], U32, name="x_all", align_bytes=64)
+        nc.sync.dma_start(x_all[:].bitcast(I32), x_words[0].rearrange("p n r -> p (n r)").bitcast(I32))
+        for t in range(2, PACK):
+            nc.sync.dma_start(tab_win[t][:, 0:S], tab_rows[:, t, :])
+        l2 = load_list("l2", n2)
+        l3 = load_list("l3", n3)
+        gain = keep.tile([P, PACK], F32, name="gain")
+        nc.sync.dma_start(gain[:], gn.rearrange("(p t) o -> p (t o)", t=PACK))
+        w2_raw = keep.tile([P, PACK, H], F32, name="w2_raw")
+        nc.sync.dma_start(w2_raw[:], w2.rearrange("(p j) c -> p j c", j=PACK))
+        l4 = load_list("l4", n4)
+        l5 = load_list("l5", n5)
+        l6 = load_list("l6", n6)
+
+        def operand(name):
+            grouped = keep.tile([P, PACK * S], BF16, name=name + "_grouped", align_bytes=64)
+            codes = keep.tile([P, S], U32, name=name + "_codes", align_bytes=64)
+            scales = keep.tile([P, S], U8, name=name + "_scales", align_bytes=64)
+            return grouped, codes, scales
+
+        def quantise(op, lo, hi):
+            nc.vector.quantize_mx(out=op[1][:, lo:hi].bitcast(FP8X4), scales=op[2][:, lo:hi], in_=op[0][:, PACK * lo : PACK * hi])
+
+        def deal_weight(copy, op, raw, lo, hi):
+            copy(op[0][:].rearrange("p (t m j) -> p m j t", t=PACK, j=PACK)[:, lo:hi], raw[:].rearrange("p j (m t) -> p m j t", t=PACK)[:, lo:hi])
+
+        def interleave_views(op, planes, lo, hi):
+            return (op[0][:, PACK * lo : PACK * hi].rearrange("p (c i t) -> p c t i", i=4, t=PACK), planes[:, :, lo:hi].rearrange("p t (c i) -> p c t i", i=4))
+
+        def banks(tag):
+            return [psum.tile([P, S], F32, name="%s%d" % (tag, t)) for t in range(PACK)]
+
+        def product(bank, weight, moving, lo, hi):
+            for t in range(PACK):
+                cols = slice(P * t, P * (t + 1))
+                nc.tensor.matmul_mx(out=bank[t][:, lo:hi], lhsT=weight[1][:, cols].bitcast(FP8X4), lhsT_scale=weight[2][:, cols],
+                                    rhs=moving[1][:, lo:hi].bitcast(FP8X4), rhs_scale=moving[2][:, lo:hi], start=True, stop=True)
+
+        def planes(name, dtype):
+            return keep.tile([P, PACK, S], dtype, name=name, align_bytes=64)
+
+        halves = [(0, S // 2), (S // 2, S)]
+        tabg = planes("tabg", F32)
+        for t in range(2):
+            nc.vector.tensor_copy(tabg[:, t, :], tab_win[t][:].indirect(l1[:]))
+        w1_q = operand("w1")
+        deal_weight(nc.vector.tensor_copy, w1_q, w1_raw, 0, 64)
+        deal_weight(nc.scalar.copy, w1_q, w1_raw, 64, 128)
+        quantise(w1_q, 0, S)
+        xs = keep.tile([P, S], U8, name="xs", align_bytes=64)
+        nc.vector.tensor_copy(xs[:], x_bytes[:].indirect(l_offs[:]))
+        xw = keep.tile([P, S], U32, name="xw", align_bytes=64)
+        nc.vector.tensor_copy(xw[:], x_all[:].indirect(l_offs[:]))
+        y_bank = banks("first")
+        product(y_bank, w1_q, (None, xw, xs), 0, S)
+        for t in range(2, PACK):
+            nc.vector.tensor_copy(tabg[:, t, :], tab_win[t][:].indirect(l1[:]))
+
+        y_win = tiles("y_win", WIN, F32)
+        sig = tiles("sig", S, F32)
+        s_win = tiles("s_win", WIN, F32)
+        s_dup = tiles("s_dup", S, F32)
+        u = planes("u", F32)
+        v = planes("v", F32)
+        zb = planes("zb", BF16)
+
+        for t in range(PACK):
+            nc.scalar.copy(y_win[t][:, 0:S], y_bank[t][:])
+            nc.vector.tensor_copy(v[:, t, :], y_win[t][:].indirect(l2[:]))
+            nc.gpsimd.tensor_tensor(u[:, t, :], y_win[t][:, 0:S], tabg[:, t, :], ALU.add)
+        for t in range(PACK):
+            nc.scalar.activation(sig[t][:], y_win[t][:].indirect(l3[:]), ACT.Sigmoid)
+            nc.vector.scalar_tensor_tensor(s_win[t][:, 0:S], y_bank[t][:], gain[:, t : t + 1], sig[t][:], ALU.mult, ALU.mult)
+            nc.sync.dma_start(s_dup[t][:], s_win[t][:, 0:S])
+        w2_q = operand("w2")
+        deal_weight(nc.scalar.copy, w2_q, w2_raw, 0, P)
+        quantise(w2_q, 0, S)
+        z_q = operand("z")
+        a_bank = banks("second")
+        for lo, hi in halves:
+            nc.vector.tensor_tensor(v[:, :, lo:hi], u[:, :, lo:hi], v[:, :, lo:hi], ALU.max)
+            for t in range(PACK):
+                nc.scalar.activation(zb[:, t, lo:hi], v[:, t, lo:hi], ACT.Copy, scale=gain[:, t : t + 1])
+            dst, src = interleave_views(z_q, zb, lo, hi)
+            nc.scalar.copy(dst, src)
+            quantise(z_q, lo, hi)
+            product(a_bank, w2_q, z_q, lo, hi)
+        d = u
+        for t in range(PACK):
+            nc.vector.tensor_tensor(d[:, t, :], s_win[t][:].indirect(l4[:]), s_dup[t][:], ALU.subtract)
+        a_win = tiles("a_win", WIN, F32)
+        a_sum = tiles("a_sum", S, F32)
+        for t in range(PACK):
+            nc.scalar.copy(a_win[t][:, 0:S], a_bank[t][:])
+            nc.vector.tensor_copy(a_sum[t][:], a_win[t][:].indirect(l5[:]))
+            nc.gpsimd.tensor_tensor(a_sum[t][:], a_sum[t][:], a_win[t][:, 0:S], ALU.add)
+        z2_q = operand("z2")
+        b_bank = banks("first")
+        for lo, hi in halves:
+            dst, src = interleave_views(z2_q, d, lo, hi)
+            nc.scalar.activation(dst, src, ACT.Copy, scale=-1.0)
+            quantise(z2_q, lo, hi)
+            product(b_bank, w2_q, z2_q, lo, hi)
+        b_win = tiles("b_win", WIN, F32)
+        b_dup = tiles("b_dup", S, F32)
+        for t in range(PACK):
+            nc.scalar.copy(b_win[t][:, 0:S], b_bank[t][:])
+            nc.scalar.copy(b_dup[t][:], b_bank[t][:])
+        b_sum = tiles("b_sum", S, F32)
+        gate = tiles("gate", S, F32)
+        out_rows = out.rearrange("(p t) c -> p t c", t=PACK)
+        for t in range(PACK):
+            nc.vector.tensor_tensor(b_sum[t][:], b_win[t][:].indirect(l6[:]), b_dup[t][:], ALU.add)
+            nc.scalar.activation(gate[t][:], b_sum[t][:], ACT.Sigmoid)
+            nc.vector.tensor_tensor(gate[t][:], a_sum[t][:], gate[t][:], ALU.mult)
+            nc.sync.dma_start(out_rows[:, t, :], gate[t][:])

@@ -40,22 +40,22 @@ def tile_picked_tietriebkindhopg_none_p_kernel(tc, x_words, x_scales, w1, tab, g
         nc.scalar.activation(warm[:, 1:2], warm[:, 0:1], ACT.Sigmoid)
 
         x_bytes = keep.tile([P, T], U8, name="x_bytes", align_bytes=64)
-        nc.vector.memset(x_bytes[:].bitcast(I32), 0)
+        nc.gpsimd.memset(x_bytes[:].bitcast(I32), 0)
 
         l1 = load_list("l1", n1)
         tab_win = tiles("tab_win", WIN, F32)
         tab_rows = tab.rearrange("(p t) c -> p t c", t=PACK)
-        for t in range(2):
+        nc.sync.dma_start(tab_win[0][:, 0:S], tab_rows[:, 0, :])
+        l_offs = load_list("l_offs", offs)
+        for q in range(4):
+            nc.scalar.dma_start(x_bytes[32 * q : 32 * q + 4, :].bitcast(I32), x_scales[0, 4 * q : 4 * q + 4, :].bitcast(I32))
+        for t in range(1, 3):
             nc.sync.dma_start(tab_win[t][:, 0:S], tab_rows[:, t, :])
         w1_raw = keep.tile([P, PACK, H], F32, name="w1_raw")
         nc.sync.dma_start(w1_raw[:], w1.rearrange("(p j) c -> p j c", j=PACK))
-        l_offs = load_list("l_offs", offs)
-        for q in range(4):
-            nc.sync.dma_start(x_bytes[32 * q : 32 * q + 4, :].bitcast(I32), x_scales[0, 4 * q : 4 * q + 4, :].bitcast(I32))
         x_all = keep.tile([P, T], U32, name="x_all", align_bytes=64)
         nc.sync.dma_start(x_all[:].bitcast(I32), x_words[0].rearrange("p n r -> p (n r)").bitcast(I32))
-        for t in range(2, PACK):
-            nc.sync.dma_start(tab_win[t][:, 0:S], tab_rows[:, t, :])
+        nc.sync.dma_start(tab_win[3][:, 0:S], tab_rows[:, 3, :])
         l2 = load_list("l2", n2)
         l3 = load_list("l3", n3)
         gain = keep.tile([P, PACK], F32, name="gain")
@@ -66,8 +66,10 @@ def tile_picked_tietriebkindhopg_none_p_kernel(tc, x_words, x_scales, w1, tab, g
         l5 = load_list("l5", n5)
         l6 = load_list("l6", n6)
 
-        def operand(name):
-            grouped = keep.tile([P, PACK * S], BF16, name=name + "_grouped", align_bytes=64)
+        def operand(name, grouped=None):
+            if grouped is None:
+                own = keep.tile([P, PACK * S], BF16, name=name + "_grouped", align_bytes=64)
+                grouped = own[:]
             codes = keep.tile([P, S], U32, name=name + "_codes", align_bytes=64)
             scales = keep.tile([P, S], U8, name=name + "_scales", align_bytes=64)
             return grouped, codes, scales
@@ -75,8 +77,11 @@ def tile_picked_tietriebkindhopg_none_p_kernel(tc, x_words, x_scales, w1, tab, g
         def quantise(op, lo, hi):
             nc.vector.quantize_mx(out=op[1][:, lo:hi].bitcast(FP8X4), scales=op[2][:, lo:hi], in_=op[0][:, PACK * lo : PACK * hi])
 
-        def deal_weight(copy, op, raw, lo, hi):
-            copy(op[0][:].rearrange("p (t m j) -> p m j t", t=PACK, j=PACK)[:, lo:hi], raw[:].rearrange("p j (m t) -> p m j t", t=PACK)[:, lo:hi])
+        def deal_weight(op, raw):
+            dst = op[0].rearrange("p (t m j) -> p m j t", t=PACK, j=PACK)
+            src = raw[:].rearrange("p j (m t) -> p m j t", t=PACK)
+            nc.gpsimd.tensor_scalar(dst[:, :, :, 0], src[:, :, :, 0], 1.0, 0.0, ALU.mult, ALU.add)
+            nc.scalar.copy(dst[:, :, :, 1:PACK], src[:, :, :, 1:PACK])
 
         def interleave_views(op, planes, lo, hi):
             return (op[0][:, PACK * lo : PACK * hi].rearrange("p (c i t) -> p c t i", i=4, t=PACK), planes[:, :, lo:hi].rearrange("p t (c i) -> p c t i", i=4))
@@ -95,11 +100,10 @@ def tile_picked_tietriebkindhopg_none_p_kernel(tc, x_words, x_scales, w1, tab, g
 
         halves = [(0, S // 2), (S // 2, S)]
         tabg = planes("tabg", F32)
-        for t in range(2):
+        for t in range(3):
             nc.vector.tensor_copy(tabg[:, t, :], tab_win[t][:].indirect(l1[:]))
         w1_q = operand("w1")
-        deal_weight(nc.vector.tensor_copy, w1_q, w1_raw, 0, 64)
-        deal_weight(nc.scalar.copy, w1_q, w1_raw, 64, 128)
+        deal_weight(w1_q, w1_raw)
         quantise(w1_q, 0, S)
         xs = keep.tile([P, S], U8, name="xs", align_bytes=64)
         nc.vector.tensor_copy(xs[:], x_bytes[:].indirect(l_offs[:]))
@@ -107,14 +111,16 @@ def tile_picked_tietriebkindhopg_none_p_kernel(tc, x_words, x_scales, w1, tab, g
         nc.vector.tensor_copy(xw[:], x_all[:].indirect(l_offs[:]))
         y_bank = banks("first")
         product(y_bank, w1_q, (None, xw, xs), 0, S)
-        for t in range(2, PACK):
+        for t in range(3, PACK):
             nc.vector.tensor_copy(tabg[:, t, :], tab_win[t][:].indirect(l1[:]))
 
         y_win = tiles("y_win", WIN, F32)
         sig = tiles("sig", S, F32)
         s_win = tiles("s_win", WIN, F32)
         s_dup = tiles("s_dup", S, F32)
-        u = planes("u", F32)
+        ud = keep.tile([P, 6 * S], F32, name="ud", align_bytes=64)
+        u = ud[:, 0 : 4 * S].rearrange("p (t c) -> p t c", t=PACK)
+        d = ud[:, 2 * S : 6 * S].rearrange("p (t c) -> p t c", t=PACK)
         v = planes("v", F32)
         zb = planes("zb", BF16)
 
@@ -127,9 +133,9 @@ def tile_picked_tietriebkindhopg_none_p_kernel(tc, x_words, x_scales, w1, tab, g
             nc.vector.scalar_tensor_tensor(s_win[t][:, 0:S], y_bank[t][:], gain[:, t : t + 1], sig[t][:], ALU.mult, ALU.mult)
             nc.sync.dma_start(s_dup[t][:], s_win[t][:, 0:S])
         w2_q = operand("w2")
-        deal_weight(nc.scalar.copy, w2_q, w2_raw, 0, P)
+        deal_weight(w2_q, w2_raw)
         quantise(w2_q, 0, S)
-        z_q = operand("z")
+        z_q = operand("z", ud[:, 4 * S : 6 * S].bitcast(BF16))
         a_bank = banks("second")
         for lo, hi in halves:
             nc.vector.tensor_tensor(v[:, :, lo:hi], u[:, :, lo:hi], v[:, :, lo:hi], ALU.max)
@@ -139,22 +145,34 @@ def tile_picked_tietriebkindhopg_none_p_kernel(tc, x_words, x_scales, w1, tab, g
             nc.scalar.copy(dst, src)
             quantise(z_q, lo, hi)
             product(a_bank, w2_q, z_q, lo, hi)
-        d = u
         for t in range(PACK):
             nc.vector.tensor_tensor(d[:, t, :], s_win[t][:].indirect(l4[:]), s_dup[t][:], ALU.subtract)
         a_win = tiles("a_win", WIN, F32)
-        a_sum = tiles("a_sum", S, F32)
-        for t in range(PACK):
+        a_all = keep.tile([P, PACK * S], F32, name="a_all", align_bytes=64)
+        a_sum = [a_all[:, t * S : (t + 1) * S] for t in range(PACK)]
+
+        def a_copy(t):
             nc.scalar.copy(a_win[t][:, 0:S], a_bank[t][:])
-            nc.vector.tensor_copy(a_sum[t][:], a_win[t][:].indirect(l5[:]))
-            nc.gpsimd.tensor_tensor(a_sum[t][:], a_sum[t][:], a_win[t][:, 0:S], ALU.add)
-        z2_q = operand("z2")
+
+        def a_step(t):
+            nc.vector.tensor_copy(a_sum[t], a_win[t][:].indirect(l5[:]))
+            if t < PACK - 1:
+                nc.gpsimd.tensor_tensor(a_sum[t], a_sum[t], a_win[t][:, 0:S], ALU.add)
+            else:
+                nc.vector.tensor_tensor(a_sum[t], a_bank[t][:], a_sum[t], ALU.add)
+
+        z2_q = operand("z2", a_all[:, 2 * S : 4 * S].bitcast(BF16))
         b_bank = banks("first")
-        for lo, hi in halves:
+        for t in range(2):
+            a_copy(t)
+            a_step(t)
+        for h, (lo, hi) in enumerate(halves):
             dst, src = interleave_views(z2_q, d, lo, hi)
             nc.scalar.activation(dst, src, ACT.Copy, scale=-1.0)
             quantise(z2_q, lo, hi)
             product(b_bank, w2_q, z2_q, lo, hi)
+            a_copy(2 + h)
+            a_step(2 + h)
         b_win = tiles("b_win", WIN, F32)
         b_dup = tiles("b_dup", S, F32)
         for t in range(PACK):
@@ -166,5 +184,6 @@ def tile_picked_tietriebkindhopg_none_p_kernel(tc, x_words, x_scales, w1, tab, g
         for t in range(PACK):
             nc.vector.tensor_tensor(b_sum[t][:], b_win[t][:].indirect(l6[:]), b_dup[t][:], ALU.add)
             nc.scalar.activation(gate[t][:], b_sum[t][:], ACT.Sigmoid)
-            nc.vector.tensor_tensor(gate[t][:], a_sum[t][:], gate[t][:], ALU.mult)
-            nc.sync.dma_start(out_rows[:, t, :], gate[t][:])
+            for lo, hi in halves if t == PACK - 1 else [(0, S)]:
+                nc.vector.tensor_tensor(gate[t][:, lo:hi], a_sum[t][:, lo:hi], gate[t][:, lo:hi], ALU.mult)
+                nc.sync.dma_start(out_rows[:, t, lo:hi], gate[t][:, lo:hi])

@@ -36,30 +36,30 @@ def tile_picked_tietriebkindhopg_none_p_kernel(tc, x_words, x_scales, w1, tab, g
             return [keep.tile([P, width], dtype, name="%s%d" % (name, t), align_bytes=64) for t in range(PACK)]
 
         warm = keep.tile([P, 8], F32, name="warm")
-        nc.vector.memset(warm[:, 0:1], 0.0)
+        nc.gpsimd.memset(warm[:, 0:1], 0.0)
         nc.scalar.activation(warm[:, 1:2], warm[:, 0:1], ACT.Sigmoid)
 
         x_bytes = keep.tile([P, T], U8, name="x_bytes", align_bytes=64)
-        nc.gpsimd.memset(x_bytes[:].bitcast(I32), 0)
+        nc.vector.memset(x_bytes[:].bitcast(I32), 0)
 
         l1 = load_list("l1", n1)
         tab_win = tiles("tab_win", WIN, F32)
         tab_rows = tab.rearrange("(p t) c -> p t c", t=PACK)
-        nc.sync.dma_start(tab_win[0][:, 0:S], tab_rows[:, 0, :])
-        l_offs = load_list("l_offs", offs)
-        for q in range(4):
-            nc.scalar.dma_start(x_bytes[32 * q : 32 * q + 4, :].bitcast(I32), x_scales[0, 4 * q : 4 * q + 4, :].bitcast(I32))
-        for t in range(1, 3):
+        for t in range(2):
             nc.sync.dma_start(tab_win[t][:, 0:S], tab_rows[:, t, :])
+        for q in range(4):
+            nc.sync.dma_start(x_bytes[32 * q : 32 * q + 4, :].bitcast(I32), x_scales[0, 4 * q : 4 * q + 4, :].bitcast(I32))
+        nc.sync.dma_start(tab_win[2][:, 0:S], tab_rows[:, 2, :])
         w1_raw = keep.tile([P, PACK, H], F32, name="w1_raw")
         nc.sync.dma_start(w1_raw[:], w1.rearrange("(p j) c -> p j c", j=PACK))
+        l_offs = load_list("l_offs", offs)
         x_all = keep.tile([P, T], U32, name="x_all", align_bytes=64)
         nc.sync.dma_start(x_all[:].bitcast(I32), x_words[0].rearrange("p n r -> p (n r)").bitcast(I32))
+        gain = keep.tile([P, PACK], F32, name="gain")
+        nc.sync.dma_start(gain[:], gn.rearrange("(p t) o -> p (t o)", t=PACK))
         nc.sync.dma_start(tab_win[3][:, 0:S], tab_rows[:, 3, :])
         l2 = load_list("l2", n2)
         l3 = load_list("l3", n3)
-        gain = keep.tile([P, PACK], F32, name="gain")
-        nc.sync.dma_start(gain[:], gn.rearrange("(p t) o -> p (t o)", t=PACK))
         w2_raw = keep.tile([P, PACK, H], F32, name="w2_raw")
         nc.sync.dma_start(w2_raw[:], w2.rearrange("(p j) c -> p j c", j=PACK))
         l4 = load_list("l4", n4)
@@ -77,11 +77,8 @@ def tile_picked_tietriebkindhopg_none_p_kernel(tc, x_words, x_scales, w1, tab, g
         def quantise(op, lo, hi):
             nc.vector.quantize_mx(out=op[1][:, lo:hi].bitcast(FP8X4), scales=op[2][:, lo:hi], in_=op[0][:, PACK * lo : PACK * hi])
 
-        def deal_weight(op, raw):
-            dst = op[0].rearrange("p (t m j) -> p m j t", t=PACK, j=PACK)
-            src = raw[:].rearrange("p j (m t) -> p m j t", t=PACK)
-            nc.gpsimd.tensor_scalar(dst[:, :, :, 0], src[:, :, :, 0], 1.0, 0.0, ALU.mult, ALU.add)
-            nc.scalar.copy(dst[:, :, :, 1:PACK], src[:, :, :, 1:PACK])
+        def deal_weight(copy, op, raw, lo, hi):
+            copy(op[0].rearrange("p (t m j) -> p m j t", t=PACK, j=PACK)[:, lo:hi], raw[:].rearrange("p j (m t) -> p m j t", t=PACK)[:, lo:hi])
 
         def interleave_views(op, planes, lo, hi):
             return (op[0][:, PACK * lo : PACK * hi].rearrange("p (c i t) -> p c t i", i=4, t=PACK), planes[:, :, lo:hi].rearrange("p t (c i) -> p c t i", i=4))
@@ -103,7 +100,8 @@ def tile_picked_tietriebkindhopg_none_p_kernel(tc, x_words, x_scales, w1, tab, g
         for t in range(3):
             nc.vector.tensor_copy(tabg[:, t, :], tab_win[t][:].indirect(l1[:]))
         w1_q = operand("w1")
-        deal_weight(w1_q, w1_raw)
+        deal_weight(nc.vector.tensor_copy, w1_q, w1_raw, 0, 64)
+        deal_weight(nc.scalar.copy, w1_q, w1_raw, 64, 128)
         quantise(w1_q, 0, S)
         xs = keep.tile([P, S], U8, name="xs", align_bytes=64)
         nc.vector.tensor_copy(xs[:], x_bytes[:].indirect(l_offs[:]))
@@ -133,7 +131,7 @@ def tile_picked_tietriebkindhopg_none_p_kernel(tc, x_words, x_scales, w1, tab, g
             nc.vector.scalar_tensor_tensor(s_win[t][:, 0:S], y_bank[t][:], gain[:, t : t + 1], sig[t][:], ALU.mult, ALU.mult)
             nc.sync.dma_start(s_dup[t][:], s_win[t][:, 0:S])
         w2_q = operand("w2")
-        deal_weight(w2_q, w2_raw)
+        deal_weight(nc.scalar.copy, w2_q, w2_raw, 0, P)
         quantise(w2_q, 0, S)
         z_q = operand("z", ud[:, 4 * S : 6 * S].bitcast(BF16))
         a_bank = banks("second")

from contextlib import ExitStack

import concourse.mybir as mybir

K, T, S, H = 512, 2048, 512, 512
FLOPS = 3 * 2 * K * H * S

F32 = mybir.dt.float32
BF16 = mybir.dt.bfloat16
I32 = mybir.dt.int32
U32 = mybir.dt.uint32
U16 = mybir.dt.uint16
U8 = mybir.dt.uint8
FP8X4 = mybir.dt.float8_e4m3fn_x4
ALU = mybir.AluOpType
ACT = mybir.ActivationFunctionType

P = 128
PACK = 4
WIN = 2 * S


def tile_picked_tietriebkindhopg_none_p_kernel(tc, x_words, x_scales, w1, tab, gn, w2, offs, n1, n2, n3, n4, n5, n6, out):
    nc = tc.nc
    with ExitStack() as ctx:
        lists = ctx.enter_context(tc.tile_pool(name="lists", bufs=1))
        keep = ctx.enter_context(tc.tile_pool(name="keep", bufs=1))
        psum = ctx.enter_context(tc.psum_pool(name="psum", bufs=1))

        def load_list(name, src):
            tile = lists.tile([P, S // 16], U16, name=name)
            nc.sync.dma_start(tile[:], src)
            return tile

        def tiles(name, width, dtype):
            return [keep.tile([P, width], dtype, name="%s%d" % (name, t), align_bytes=64) for t in range(PACK)]

        warm = keep.tile([P, 8], F32, name="warm")
        nc.gpsimd.memset(warm[:, 0:1], 0.0)
        nc.scalar.activation(warm[:, 1:2], warm[:, 0:1], ACT.Sigmoid)

        x_bytes = keep.tile([P, T], U8, name="x_bytes", align_bytes=64)
        nc.vector.memset(x_bytes[:].bitcast(I32), 0)

        l1 = load_list("l1", n1)
        tab_win = tiles("tab_win", WIN, F32)
        tab_rows = tab.rearrange("(p t) c -> p t c", t=PACK)
        for t in range(2):
            nc.sync.dma_start(tab_win[t][:, 0:S], tab_rows[:, t, :])
        for q in range(4):
            nc.sync.dma_start(x_bytes[32 * q : 32 * q + 4, :].bitcast(I32), x_scales[0, 4 * q : 4 * q + 4, :].bitcast(I32))
        nc.sync.dma_start(tab_win[2][:, 0:S], tab_rows[:, 2, :])
        w1_raw = keep.tile([P, PACK, H], F32, name="w1_raw")
        nc.sync.dma_start(w1_raw[:], w1.rearrange("(p j) c -> p j c", j=PACK))
        l_offs = load_list("l_offs", offs)
        x_all = keep.tile([P, T], U32, name="x_all", align_bytes=64)
        nc.sync.dma_start(x_all[:].bitcast(I32), x_words[0].rearrange("p n r -> p (n r)").bitcast(I32))
        gain = keep.tile([P, PACK], F32, name="gain")
        nc.sync.dma_start(gain[:], gn.rearrange("(p t) o -> p (t o)", t=PACK))
        nc.sync.dma_start(tab_win[3][:, 0:S], tab_rows[:, 3, :])
        l2 = load_list("l2", n2)
        l3 = load_list("l3", n3)
        w2_raw = keep.tile([P, PACK, H], F32, name="w2_raw")
        nc.sync.dma_start(w2_raw[:], w2.rearrange("(p j) c -> p j c", j=PACK))
        l4 = load_list("l4", n4)
        l5 = load_list("l5", n5)
        l6 = load_list("l6", n6)

        def operand(name, grouped=None):
            if grouped is None:
                own = keep.tile([P, PACK * S], BF16, name=name + "_grouped", align_bytes=64)
                grouped = own[:]
            codes = keep.tile([P, S], U32, name=name + "_codes", align_bytes=64)
            scales = keep.tile([P, S], U8, name=name + "_scales", align_bytes=64)
            return grouped, codes, scales

        def quantise(op, lo, hi):
            nc.vector.quantize_mx(out=op[1][:, lo:hi].bitcast(FP8X4), scales=op[2][:, lo:hi], in_=op[0][:, PACK * lo : PACK * hi])

        def deal_weight(copy, op, raw, lo, hi):
            copy(op[0].rearrange("p (t m j) -> p m j t", t=PACK, j=PACK)[:, lo:hi], raw[:].rearrange("p j (m t) -> p m j t", t=PACK)[:, lo:hi])

        def interleave_views(op, planes, lo, hi):
            return (op[0][:, PACK * lo : PACK * hi].rearrange("p (c i t) -> p c t i", i=4, t=PACK), planes[:, :, lo:hi].rearrange("p t (c i) -> p c t i", i=4))

        def banks(tag):
            return [psum.tile([P, S], F32, name="%s%d" % (tag, t)) for t in range(PACK)]

        def product(bank, weight, moving, lo, hi):
            for t in range(PACK):
                cols = slice(P * t, P * (t + 1))
                nc.tensor.matmul_mx(out=bank[t][:, lo:hi], lhsT=weight[1][:, cols].bitcast(FP8X4), lhsT_scale=weight[2][:, cols],
                                    rhs=moving[1][:, lo:hi].bitcast(FP8X4), rhs_scale=moving[2][:, lo:hi], start=True, stop=True)

        def planes(name, dtype):
            return keep.tile([P, PACK, S], dtype, name=name, align_bytes=64)

        halves = [(0, S // 2), (S // 2, S)]
        tabg = planes("tabg", F32)
        for t in range(3):
            nc.vector.tensor_copy(tabg[:, t, :], tab_win[t][:].indirect(l1[:]))
        w1_q = operand("w1")
        deal_weight(nc.vector.tensor_copy, w1_q, w1_raw, 0, 64)
        deal_weight(nc.scalar.copy, w1_q, w1_raw, 64, 128)
        quantise(w1_q, 0, S)
        xs = keep.tile([P, S], U8, name="xs", align_bytes=64)
        nc.vector.tensor_copy(xs[:], x_bytes[:].indirect(l_offs[:]))
        xw = keep.tile([P, S], U32, name="xw", align_bytes=64)
        nc.vector.tensor_copy(xw[:], x_all[:].indirect(l_offs[:]))
        y_bank = banks("first")
        product(y_bank, w1_q, (None, xw, xs), 0, S)
        for t in range(3, PACK):
            nc.vector.tensor_copy(tabg[:, t, :], tab_win[t][:].indirect(l1[:]))

        y_win = tiles("y_win", WIN, F32)
        sig = tiles("sig", S, F32)
        s_win = tiles("s_win", WIN, F32)
        s_dup = tiles("s_dup", S, F32)
        ud = keep.tile([P, 6 * S], F32, name="ud", align_bytes=64)
        u = ud[:, 0 : 4 * S].rearrange("p (t c) -> p t c", t=PACK)
        d = ud[:, 2 * S : 6 * S].rearrange("p (t c) -> p t c", t=PACK)
        v = planes("v", F32)
        zb = planes("zb", BF16)

        for t in range(PACK):
            nc.scalar.copy(y_win[t][:, 0:S], y_bank[t][:])
            nc.vector.tensor_copy(v[:, t, :], y_win[t][:].indirect(l2[:]))
            nc.gpsimd.tensor_tensor(u[:, t, :], y_win[t][:, 0:S], tabg[:, t, :], ALU.add)
        for t in range(PACK):
            nc.scalar.activation(sig[t][:], y_win[t][:].indirect(l3[:]), ACT.Sigmoid)
            nc.vector.scalar_tensor_tensor(s_win[t][:, 0:S], y_bank[t][:], gain[:, t : t + 1], sig[t][:], ALU.mult, ALU.mult)
            nc.sync.dma_start(s_dup[t][:], s_win[t][:, 0:S])
        w2_q = operand("w2")
        deal_weight(nc.scalar.copy, w2_q, w2_raw, 0, P)
        quantise(w2_q, 0, S)
        z_q = operand("z", ud[:, 4 * S : 6 * S].bitcast(BF16))
        a_bank = banks("second")
        for lo, hi in halves:
            nc.vector.tensor_tensor(v[:, :, lo:hi], u[:, :, lo:hi], v[:, :, lo:hi], ALU.max)
            for t in range(PACK):
                nc.scalar.activation(zb[:, t, lo:hi], v[:, t, lo:hi], ACT.Copy, scale=gain[:, t : t + 1])
            dst, src = interleave_views(z_q, zb, lo, hi)
            nc.scalar.copy(dst, src)
            quantise(z_q, lo, hi)
            product(a_bank, w2_q, z_q, lo, hi)
        for t in range(PACK):
            nc.vector.tensor_tensor(d[:, t, :], s_win[t][:].indirect(l4[:]), s_dup[t][:], ALU.subtract)
        a_win = tiles("a_win", WIN, F32)
        a_all = keep.tile([P, PACK * S], F32, name="a_all", align_bytes=64)
        a_sum = [a_all[:, t * S : (t + 1) * S] for t in range(PACK)]

        def a_copy(t):
            nc.scalar.copy(a_win[t][:, 0:S], a_bank[t][:])

        def a_step(t):
            nc.vector.tensor_copy(a_sum[t], a_win[t][:].indirect(l5[:]))
            if t < PACK - 1:
                nc.gpsimd.tensor_tensor(a_sum[t], a_sum[t], a_win[t][:, 0:S], ALU.add)
            else:
                nc.vector.tensor_tensor(a_sum[t], a_bank[t][:], a_sum[t], ALU.add)

        z2_q = operand("z2", a_all[:, 2 * S : 4 * S].bitcast(BF16))
        b_bank = banks("first")
        for t in range(2):
            a_copy(t)
            a_step(t)
        for h, (lo, hi) in enumerate(halves):
            dst, src = interleave_views(z2_q, d, lo, hi)
            nc.scalar.activation(dst, src, ACT.Copy, scale=-1.0)
            quantise(z2_q, lo, hi)
            product(b_bank, w2_q, z2_q, lo, hi)
            a_copy(2 + h)
            a_step(2 + h)
        b_win = tiles("b_win", WIN, F32)
        b_dup = tiles("b_dup", S, F32)
        for t in range(PACK):
            nc.scalar.copy(b_win[t][:, 0:S], b_bank[t][:])
            nc.scalar.copy(b_dup[t][:], b_bank[t][:])
        b_sum = tiles("b_sum", S, F32)
        gate = tiles("gate", S, F32)
        out_rows = out.rearrange("(p t) c -> p t c", t=PACK)
        for t in range(PACK):
            nc.vector.tensor_tensor(b_sum[t][:], b_win[t][:].indirect(l6[:]), b_dup[t][:], ALU.add)
            nc.scalar.activation(gate[t][:], b_sum[t][:], ACT.Sigmoid)
            for lo, hi in halves if t == PACK - 1 else [(0, S)]:
                nc.vector.tensor_tensor(gate[t][:, lo:hi], a_sum[t][:, lo:hi], gate[t][:, lo:hi], ALU.mult)
                nc.sync.dma_start(out_rows[:, t, lo:hi], gate[t][:, lo:hi])
